import numpy as np
import ml_dtypes


def mxq(x, axis, fmt="e4m3"):
    dtype, down = {"e4m3": (ml_dtypes.float8_e4m3fn, 7), "e5m2": (ml_dtypes.float8_e5m2, 14)}[fmt]
    v = np.moveaxis(np.asarray(x, np.float32).astype(ml_dtypes.bfloat16).astype(np.float64), axis, -1)
    blocks = v.reshape(v.shape[:-1] + (-1, 32))
    amax = np.abs(blocks).max(-1, keepdims=True)
    byte = np.maximum(np.where(amax > 0, np.frexp(amax)[1] - 1 + 127, 0) - down, 1)
    scale = np.exp2(byte - 127.0)
    codes = (blocks / scale).astype(np.float32).astype(dtype).astype(np.float64)
    return np.moveaxis((codes * scale).reshape(v.shape), -1, axis)


WIDE = False


def mx_kscale(k):
    if not WIDE:
        return np.ones(k)
    levels = np.array([10, -10, 5, -5, 0])
    if k % 512:
        return np.exp2(np.random.permutation(np.resize(levels, k // 32))).repeat(32)
    a = np.empty((k // 512, 16))
    for p in range(k // 512):
        a[p, :8] = np.random.permutation(np.resize(levels, 8))
        for g in range(8):
            far = levels[np.abs(levels - a[p, g]) >= 10]
            a[p, g + 8] = far[np.random.randint(len(far))]
    return np.exp2(a.ravel()).repeat(32)


def f64(x):
    return np.asarray(x).astype(np.float64)


def striped(idx):
    return np.tile(idx.reshape(-1, 16).T, (8, 1)).astype(np.uint16)


def unstriped(offs):
    return offs[:16].T.reshape(-1).astype(np.int64)


def pack_weight(w):
    k, n = w.shape
    w = f64(np.asarray(w, np.float32).astype(ml_dtypes.bfloat16)).reshape(k // 32, 32, n)
    amax = np.abs(w).max(1)
    byte = np.clip(np.where(amax > 0, np.frexp(amax)[1] - 1 + 127 - 7, 1), 1, 254)
    scaled = (w * np.exp2(127.0 - byte)[:, None, :]).reshape(k, n).astype(np.float32)
    words = np.ascontiguousarray(scaled.reshape(k // 512, 128, 4, n).transpose(0, 1, 3, 2)).astype(ml_dtypes.float8_e4m3fn).view(np.uint8)
    return words, np.ascontiguousarray(byte.astype(np.uint8).reshape(k // 512, 16, n))


def unpack_weight(words, scales):
    g, p, n, _ = words.shape
    vals = np.ascontiguousarray(words).view(ml_dtypes.float8_e4m3fn).astype(np.float64) * np.repeat(np.exp2(scales.astype(np.float64) - 127.0), 8, axis=1)[..., None]
    return vals.transpose(0, 1, 3, 2).reshape(g * 512, n)


def relu(v):
    return np.maximum(v, 0.0)


def sigmoid(v):
    return 1.0 / (1.0 + np.exp(-np.maximum(v, -700.0)))


K, T, S, D, N, H, V, U = 512, 4096, 1024, 4, 128, 512, 256, 512


def setup_inputs():
    n = np.random.standard_normal
    s = mx_kscale(K)[:, None]
    u = mx_kscale(H)
    packed_xT = pack_weight(n((K, T)) * s)
    return {
        "x_words": packed_xT[0],
        "x_scales": packed_xT[1],
        "w1": (n((K, H)) / np.sqrt(K) / s).astype(np.float32),
        "w2": (n((K, H)) / np.sqrt(K) / s).astype(np.float32),
        "qry": (n((H, U))).astype(np.float32),
        "unit": (np.random.uniform(0.6, 1.4, (H, 1)) * u[:, None]).astype(np.float32),
        "w3": (n((H, N)) / np.sqrt(H) / u[:, None]).astype(np.float32),
        "old": (n((N, U))).astype(np.float32),
        "offs": striped(np.random.permutation(T)[:S]),
        "pg": striped(np.random.permutation(np.concatenate([np.arange(V), np.random.randint(0, V, U - V)]))),
    }


def reference(x_words, x_scales, w1, w2, qry, unit, w3, old, offs, pg):
    xq = unpack_weight(x_words, x_scales)[:, unstriped(offs)]
    yw = mxq(f64(w2), 0, "e4m3").T @ xq
    ys = mxq(f64(w1), 0, "e4m3").T @ xq
    sc = sigmoid(yw) * relu(ys)
    best = sc.reshape(len(sc), -1, D).max(axis=2)
    tp = best[:, unstriped(pg)]
    mt = tp * (np.tanh(f64(qry)))
    hid = f64(unit) * mt
    rr = mxq(f64(w3), 0, "e4m3").T @ mxq(hid, 0, "e4m3")
    return rr + f64(old)

@@ -1,0 +1,200 @@
+from contextlib import ExitStack
+
+import concourse.mybir as mybir
+
+K, T, S, D, N, H, V, U = 512, 4096, 1024, 4, 128, 512, 256, 512
+FLOPS = 2 * K * H * S * 2 + 2 * H * N * U
+
+F32 = mybir.dt.float32
+BF16 = mybir.dt.bfloat16
+I32 = mybir.dt.int32
+U32 = mybir.dt.uint32
+U16 = mybir.dt.uint16
+U8 = mybir.dt.uint8
+FP8X4 = mybir.dt.float8_e4m3fn_x4
+ALU = mybir.AluOpType
+ACT = mybir.ActivationFunctionType
+
+P = 128
+PACK = 4
+BANK = 512
+WINDOW = 704
+CHUNK = 256
+
+
+def tile_picked_yxindx_tied_p_kernel(tc, x_words, x_scales, w1, w2, qry, unit, w3, old, offs, pg, out):
+    nc = tc.nc
+    with ExitStack() as ctx:
+        keep = ctx.enter_context(tc.tile_pool(name="keep", bufs=1))
+        ring = ctx.enter_context(tc.tile_pool(name="ring", bufs=2))
+        psum = ctx.enter_context(tc.psum_pool(name="psum", bufs=1))
+
+        offs_t = keep.tile([P, S // 16], U16, name="offs_t")
+        pg_t = keep.tile([P, U // 16], U16, name="pg_t")
+        words = keep.tile([P, T], I32, name="words", align_bytes=64)
+        scales = keep.tile([P, T], U8, name="scales", align_bytes=64)
+        best = keep.tile([P, (PACK - 1) * V + WINDOW], F32, name="best", align_bytes=64)
+        warm = keep.tile([P, 2], F32, name="warm")
+
+        nc.vector.memset(scales[:].bitcast(I32), 0)
+        nc.vector.memset(warm[:, 0:1], 0.0)
+        nc.vector.memset(best[:, PACK * V :], 0.0)
+        nc.scalar.activation(warm[:, 1:2], warm[:, 0:1], ACT.Sigmoid)
+
+        nc.sync.dma_start(offs_t[:], offs)
+        nc.sync.dma_start(words[:], x_words[0].rearrange("p c r -> p (c r)").bitcast(I32))
+        for q in range(4):
+            nc.gpsimd.dma_start(
+                scales[32 * q : 32 * q + 4, :].bitcast(I32), x_scales[0, 4 * q : 4 * q + 4, :].bitcast(I32)
+            )
+        w2_raw = keep.tile([P, PACK, H], F32, name="w2_raw")
+        w1_raw = keep.tile([P, PACK, H], F32, name="w1_raw")
+        qry_raw = keep.tile([P, PACK, U], F32, name="qry_raw")
+        w3_raw = keep.tile([P, PACK, N], F32, name="w3_raw")
+        unit_t = keep.tile([P, PACK], F32, name="unit_t")
+        old_t = keep.tile([P, U], F32, name="old_t")
+        nc.sync.dma_start(w2_raw[:], w2.rearrange("(p j) c -> p j c", j=PACK))
+        nc.sync.dma_start(w1_raw[:], w1.rearrange("(p j) c -> p j c", j=PACK))
+        nc.sync.dma_start(qry_raw[:], qry.rearrange("(p j) c -> p j c", j=PACK))
+        nc.sync.dma_start(unit_t[:], unit.rearrange("(p j) o -> p (j o)", j=PACK))
+        nc.sync.dma_start(pg_t[:], pg)
+        nc.sync.dma_start(w3_raw[:], w3.rearrange("(p j) c -> p j c", j=PACK))
+        nc.sync.dma_start(old_t[:], old)
+
+        x_scale = keep.tile([P, S], U8, name="x_scale", align_bytes=64)
+        x_code = keep.tile([P, S], U32, name="x_code", align_bytes=64)
+        nc.vector.tensor_copy(x_scale[:], scales[:].indirect(offs_t[:]))
+        nc.vector.tensor_copy(x_code[:], words[:].bitcast(U32).indirect(offs_t[:]))
+
+        def cast_pair(copy, raw, a, name):
+            pair = keep.tile([P, 2, P, PACK], BF16, name=name, align_bytes=64)
+            copy(
+                pair[:].rearrange("p e m j -> p m j e"),
+                raw[:].rearrange("p j (m t) -> p m j t", t=PACK)[:, :, :, 2 * a : 2 * a + 2],
+            )
+            return pair
+
+        def quantize(src, width, name):
+            code = keep.tile([P, width], U32, name=name + "_code", align_bytes=64)
+            scale = keep.tile([P, width], U8, name=name + "_scale", align_bytes=64)
+            nc.vector.quantize_mx(out=code[:].bitcast(FP8X4), scales=scale[:], in_=src)
+            return code, scale
+
+        def planes_of(raw, name):
+            pairs = [
+                cast_pair(nc.vector.tensor_copy, raw, 0, name + "_lo"),
+                cast_pair(nc.scalar.copy, raw, 1, name + "_hi"),
+            ]
+            return [
+                quantize(pairs[t // 2][:, t % 2, :, :].rearrange("p m j -> p (m j)"), P, name + "_%d" % t)
+                for t in range(PACK)
+            ]
+
+        def product(weights, h, tag, bufs):
+            code, scale = weights
+            cols = slice(h * BANK, (h + 1) * BANK)
+            acc = psum.tile([P, BANK], F32, name=tag, tag=tag, bufs=bufs)
+            nc.tensor.matmul_mx(
+                out=acc[:],
+                lhsT=code[:].bitcast(FP8X4),
+                lhsT_scale=scale[:],
+                rhs=x_code[:, cols].bitcast(FP8X4),
+                rhs_scale=x_scale[:, cols],
+                start=True,
+                stop=True,
+            )
+            return acc
+
+        w2_q = planes_of(w2_raw, "w2")
+        gates = {}
+
+        def gate(t, h):
+            yw = product(w2_q[t], h, "yw", 3)
+            gates[t, h] = keep.tile([P, BANK], F32, name="gate_%d_%d" % (t, h))
+            nc.scalar.activation(gates[t, h][:], yw[:], ACT.Sigmoid)
+
+        gate(0, 0)
+        w1_q = planes_of(w1_raw, "w1")
+        for b in range(1, 2 * PACK):
+            gate(b // 2, b % 2)
+
+        bounded = keep.tile([P, PACK, U], F32, name="bounded")
+        factor = keep.tile([P, PACK, U], F32, name="factor")
+        nc.scalar.activation(bounded[:], qry_raw[:], ACT.Tanh)
+        for t in range(PACK):
+            nc.scalar.activation(factor[:, t, :], bounded[:, t, :], ACT.Copy, scale=unit_t[:, t : t + 1])
+        w3_bf = keep.tile([P, N, PACK], BF16, name="w3_bf", align_bytes=64)
+        nc.scalar.copy(
+            w3_bf[:].rearrange("p (c i) j -> p c j i", i=2), w3_raw[:].rearrange("p j (c i) -> p c j i", i=2)
+        )
+
+        looked = keep.tile([P, PACK, U], F32, name="looked")
+        score = {}
+        half = {}
+
+        def scores(t, h):
+            if h == 0:
+                score[t] = ring.tile([P, V, D], F32, name="score")
+            ys = product(w1_q[t], h, "ys", 3)
+            nc.vector.scalar_tensor_tensor(
+                score[t][:].rearrange("p v d -> p (v d)")[:, h * BANK : (h + 1) * BANK],
+                ys[:],
+                0.0,
+                gates[t, h][:],
+                ALU.max,
+                ALU.mult,
+            )
+
+        def first_max(t):
+            half[t] = ring.tile([P, V, 2], F32, name="half")
+            nc.vector.tensor_tensor(half[t][:], score[t][:, :, 0:2], score[t][:, :, 2:4], ALU.max)
+
+        def second_max(t):
+            at = (PACK - 1 - t) * V
+            nc.vector.tensor_tensor(best[:, at : at + V], half[t][:, :, 0], half[t][:, :, 1], ALU.max)
+
+        def look_up(t):
+            at = (PACK - 1 - t) * V
+            nc.vector.tensor_copy(looked[:, t, :], best[:, at : at + WINDOW].indirect(pg_t[:]))
+
+        for t in range(PACK + 1):
+            if t < PACK:
+                scores(t, 0)
+            if t > 0:
+                first_max(t - 1)
+            if t < PACK:
+                scores(t, 1)
+            if t > 1:
+                look_up(t - 2)
+            if t > 0:
+                second_max(t - 1)
+        w3_code, w3_scale = quantize(w3_bf[:].rearrange("p n j -> p (n j)"), N, "w3")
+        look_up(PACK - 1)
+
+        chunks = range(U // CHUNK)
+        hid = []
+        for c in chunks:
+            cols = slice(c * CHUNK, (c + 1) * CHUNK)
+            hid.append(keep.tile([P, CHUNK, PACK], BF16, name="hid_%d" % c, align_bytes=64))
+            nc.vector.tensor_tensor(
+                hid[c][:].rearrange("p (c i) t -> p c t i", i=2),
+                looked[:, :, cols].rearrange("p t (c i) -> p c t i", i=2),
+                factor[:, :, cols].rearrange("p t (c i) -> p c t i", i=2),
+                ALU.mult,
+            )
+        hid_q = [quantize(hid[c][:].rearrange("p r t -> p (r t)"), CHUNK, "hid_%d" % c) for c in chunks]
+        for c in chunks:
+            cols = slice(c * CHUNK, (c + 1) * CHUNK)
+            rr = psum.tile([P, CHUNK], F32, name="rr", tag="rr", bufs=2)
+            nc.tensor.matmul_mx(
+                out=rr[:],
+                lhsT=w3_code[:].bitcast(FP8X4),
+                lhsT_scale=w3_scale[:],
+                rhs=hid_q[c][0][:].bitcast(FP8X4),
+                rhs_scale=hid_q[c][1][:],
+                start=True,
+                stop=True,
+            )
+            res = ring.tile([P, CHUNK], F32, name="res")
+            nc.vector.tensor_tensor(res[:], rr[:], old_t[:, cols], ALU.add)
+            nc.sync.dma_start(out[:, cols], res[:])

@@ -20,6 +20,8 @@ PACK = 4
 BANK = 512
 WINDOW = 704
 CHUNK = 256
+HALF = H // 2
+PLACE = {2: 0, 0: 1, 3: 2, 1: 3}
 
 
 def tile_picked_yxindx_tied_p_kernel(tc, x_words, x_scales, w1, w2, qry, unit, w3, old, offs, pg, out):
@@ -31,7 +33,7 @@ def tile_picked_yxindx_tied_p_kernel(tc, x_words, x_scales, w1, w2, qry, unit, w
 
         offs_t = keep.tile([P, S // 16], U16, name="offs_t")
         pg_t = keep.tile([P, U // 16], U16, name="pg_t")
-        words = keep.tile([P, T], I32, name="words", align_bytes=64)
+        words = keep.tile([P, T], I32, name="words", tag="words", align_bytes=64)
         scales = keep.tile([P, T], U8, name="scales", align_bytes=64)
         best = keep.tile([P, (PACK - 1) * V + WINDOW], F32, name="best", align_bytes=64)
         warm = keep.tile([P, 2], F32, name="warm")
@@ -41,135 +43,166 @@ def tile_picked_yxindx_tied_p_kernel(tc, x_words, x_scales, w1, w2, qry, unit, w
         nc.vector.memset(best[:, PACK * V :], 0.0)
         nc.scalar.activation(warm[:, 1:2], warm[:, 0:1], ACT.Sigmoid)
 
+        def load_half(w, half, name):
+            raw = keep.tile([P, PACK, HALF], F32, name=name, tag=name, align_bytes=64)
+            nc.sync.dma_start(raw[:], w.rearrange("(p j) c -> p j c", j=PACK)[:, :, half * HALF : (half + 1) * HALF])
+            return raw
+
         nc.sync.dma_start(offs_t[:], offs)
-        nc.sync.dma_start(words[:], x_words[0].rearrange("p c r -> p (c r)").bitcast(I32))
+        w2_raw = [load_half(w2, 0, "w2_raw_0")]
         for q in range(4):
-            nc.gpsimd.dma_start(
+            nc.sync.dma_start(
                 scales[32 * q : 32 * q + 4, :].bitcast(I32), x_scales[0, 4 * q : 4 * q + 4, :].bitcast(I32)
             )
-        w2_raw = keep.tile([P, PACK, H], F32, name="w2_raw")
-        w1_raw = keep.tile([P, PACK, H], F32, name="w1_raw")
+        nc.sync.dma_start(words[:], x_words[0].rearrange("p c r -> p (c r)").bitcast(I32))
+        w1_raw = [load_half(w1, 0, "w1_raw_0")]
+        w2_raw.append(load_half(w2, 1, "w2_raw_1"))
+        w1_raw.append(load_half(w1, 1, "w1_raw_1"))
         qry_raw = keep.tile([P, PACK, U], F32, name="qry_raw")
         w3_raw = keep.tile([P, PACK, N], F32, name="w3_raw")
         unit_t = keep.tile([P, PACK], F32, name="unit_t")
         old_t = keep.tile([P, U], F32, name="old_t")
-        nc.sync.dma_start(w2_raw[:], w2.rearrange("(p j) c -> p j c", j=PACK))
-        nc.sync.dma_start(w1_raw[:], w1.rearrange("(p j) c -> p j c", j=PACK))
         nc.sync.dma_start(qry_raw[:], qry.rearrange("(p j) c -> p j c", j=PACK))
         nc.sync.dma_start(unit_t[:], unit.rearrange("(p j) o -> p (j o)", j=PACK))
         nc.sync.dma_start(pg_t[:], pg)
         nc.sync.dma_start(w3_raw[:], w3.rearrange("(p j) c -> p j c", j=PACK))
         nc.sync.dma_start(old_t[:], old)
 
-        x_scale = keep.tile([P, S], U8, name="x_scale", align_bytes=64)
-        x_code = keep.tile([P, S], U32, name="x_code", align_bytes=64)
-        nc.vector.tensor_copy(x_scale[:], scales[:].indirect(offs_t[:]))
-        nc.vector.tensor_copy(x_code[:], words[:].bitcast(U32).indirect(offs_t[:]))
-
-        def cast_pair(copy, raw, a, name):
-            pair = keep.tile([P, 2, P, PACK], BF16, name=name, align_bytes=64)
+        def deal(copy, raw, slots, name, tag):
+            count = slots.stop - slots.start
+            dealt = keep.tile([P, count, HALF // PACK, PACK], BF16, name=name, tag=tag, align_bytes=64)
             copy(
-                pair[:].rearrange("p e m j -> p m j e"),
-                raw[:].rearrange("p j (m t) -> p m j t", t=PACK)[:, :, :, 2 * a : 2 * a + 2],
+                dealt[:].rearrange("p t m j -> p m j t"),
+                raw[:].rearrange("p j (m t) -> p m j t", t=PACK)[:, :, :, slots],
             )
-            return pair
+            return dealt[:].rearrange("p t m j -> p (t m j)")
 
         def quantize(src, width, name):
-            code = keep.tile([P, width], U32, name=name + "_code", align_bytes=64)
-            scale = keep.tile([P, width], U8, name=name + "_scale", align_bytes=64)
+            code = keep.tile([P, width], U32, name=name + "_code", tag=name + "_code", align_bytes=64)
+            scale = keep.tile([P, width], U8, name=name + "_scale", tag=name + "_scale", align_bytes=64)
             nc.vector.quantize_mx(out=code[:].bitcast(FP8X4), scales=scale[:], in_=src)
             return code, scale
 
-        def planes_of(raw, name):
-            pairs = [
-                cast_pair(nc.vector.tensor_copy, raw, 0, name + "_lo"),
-                cast_pair(nc.scalar.copy, raw, 1, name + "_hi"),
-            ]
-            return [
-                quantize(pairs[t // 2][:, t % 2, :, :].rearrange("p m j -> p (m j)"), P, name + "_%d" % t)
-                for t in range(PACK)
-            ]
+        x_scale = keep.tile([P, S], U8, name="x_scale", align_bytes=64)
+        x_code = {}
+
+        def pick_words(h, tag):
+            x_code[h] = keep.tile([P, BANK], U32, name="x_code_%d" % h, tag=tag, align_bytes=64)
+            part = offs_t[:, h * BANK // 16 : (h + 1) * BANK // 16]
+            nc.vector.tensor_copy(x_code[h][:], words[:].bitcast(U32).indirect(part))
+
+        def blocks(quantized):
+            code, scale = quantized
+            return [(code[:, e * P : (e + 1) * P], scale[:, e * P : (e + 1) * P]) for e in range(code.shape[1] // P)]
 
         def product(weights, h, tag, bufs):
             code, scale = weights
-            cols = slice(h * BANK, (h + 1) * BANK)
             acc = psum.tile([P, BANK], F32, name=tag, tag=tag, bufs=bufs)
             nc.tensor.matmul_mx(
                 out=acc[:],
-                lhsT=code[:].bitcast(FP8X4),
-                lhsT_scale=scale[:],
-                rhs=x_code[:, cols].bitcast(FP8X4),
-                rhs_scale=x_scale[:, cols],
+                lhsT=code.bitcast(FP8X4),
+                lhsT_scale=scale,
+                rhs=x_code[h][:].bitcast(FP8X4),
+                rhs_scale=x_scale[:, h * BANK : (h + 1) * BANK],
                 start=True,
                 stop=True,
             )
             return acc
 
-        w2_q = planes_of(w2_raw, "w2")
-        gates = {}
+        w1_q, w2_q, gates, score, pairs = [], [], {}, {}, {}
 
-        def gate(t, h):
-            yw = product(w2_q[t], h, "yw", 3)
-            gates[t, h] = keep.tile([P, BANK], F32, name="gate_%d_%d" % (t, h))
-            nc.scalar.activation(gates[t, h][:], yw[:], ACT.Sigmoid)
+        def gate(b, h):
+            yw = product(w2_q[b], h, "yw", 2)
+            nc.scalar.activation(gates[b // 2][:, 2 * (b % 2) + h, :], yw[:], ACT.Sigmoid)
 
-        gate(0, 0)
-        w1_q = planes_of(w1_raw, "w1")
-        for b in range(1, 2 * PACK):
-            gate(b // 2, b % 2)
-
-        bounded = keep.tile([P, PACK, U], F32, name="bounded")
-        factor = keep.tile([P, PACK, U], F32, name="factor")
-        nc.scalar.activation(bounded[:], qry_raw[:], ACT.Tanh)
-        for t in range(PACK):
-            nc.scalar.activation(factor[:, t, :], bounded[:, t, :], ACT.Copy, scale=unit_t[:, t : t + 1])
-        w3_bf = keep.tile([P, N, PACK], BF16, name="w3_bf", align_bytes=64)
-        nc.scalar.copy(
-            w3_bf[:].rearrange("p (c i) j -> p c j i", i=2), w3_raw[:].rearrange("p j (c i) -> p c j i", i=2)
-        )
-
-        looked = keep.tile([P, PACK, U], F32, name="looked")
-        score = {}
-        half = {}
-
-        def scores(t, h):
+        def scores(b, h):
             if h == 0:
-                score[t] = ring.tile([P, V, D], F32, name="score")
-            ys = product(w1_q[t], h, "ys", 3)
+                score[b] = ring.tile([P, V, D], F32, name="score")
+            ys = product(w1_q[b], h, "ys", 4)
             nc.vector.scalar_tensor_tensor(
-                score[t][:].rearrange("p v d -> p (v d)")[:, h * BANK : (h + 1) * BANK],
+                score[b][:].rearrange("p v d -> p (v d)")[:, h * BANK : (h + 1) * BANK],
                 ys[:],
                 0.0,
-                gates[t, h][:],
+                gates[b // 2][:, 2 * (b % 2) + h, :],
                 ALU.max,
                 ALU.mult,
             )
 
-        def first_max(t):
-            half[t] = ring.tile([P, V, 2], F32, name="half")
-            nc.vector.tensor_tensor(half[t][:], score[t][:, :, 0:2], score[t][:, :, 2:4], ALU.max)
+        def first_max(b):
+            pairs[b] = ring.tile([P, V, 2], F32, name="pairs")
+            nc.vector.tensor_tensor(pairs[b][:], score[b][:, :, 0:2], score[b][:, :, 2:4], ALU.max)
 
-        def second_max(t):
-            at = (PACK - 1 - t) * V
-            nc.vector.tensor_tensor(best[:, at : at + V], half[t][:, :, 0], half[t][:, :, 1], ALU.max)
+        def columns(t):
+            return slice(PLACE[t] * V, (PLACE[t] + 1) * V)
+
+        low, high = slice(0, P // 2), slice(P // 2, P)
+
+        def second_max(b):
+            even, odd = columns(2 * (b % 2)), columns(2 * (b % 2) + 1)
+            if b < 2:
+                nc.vector.tensor_tensor(best[:, even], pairs[b][:, :, 0], pairs[b][:, :, 1], ALU.max)
+                nc.sync.dma_start(best[low, odd], best[high, even])
+            else:
+                upper = ring.tile([P, V], F32, name="upper")
+                nc.vector.tensor_tensor(upper[:], pairs[b][:, :, 0], pairs[b][:, :, 1], ALU.max)
+                nc.sync.dma_start(best[high, even], upper[low, :])
+                nc.scalar.copy(best[high, odd], upper[high, :])
+
+        looked = keep.tile([P, PACK, U], F32, name="looked")
 
         def look_up(t):
-            at = (PACK - 1 - t) * V
+            at = PLACE[t] * V
             nc.vector.tensor_copy(looked[:, t, :], best[:, at : at + WINDOW].indirect(pg_t[:]))
 
-        for t in range(PACK + 1):
-            if t < PACK:
-                scores(t, 0)
-            if t > 0:
-                first_max(t - 1)
-            if t < PACK:
-                scores(t, 1)
-            if t > 1:
-                look_up(t - 2)
-            if t > 0:
-                second_max(t - 1)
+        whole = slice(0, PACK)
+        w2_q.extend(blocks(quantize(deal(nc.vector.tensor_copy, w2_raw[0], whole, "w2_bf_0", "w2_bf_0"), HALF, "w2_0")))
+        nc.vector.tensor_copy(x_scale[:], scales[:].indirect(offs_t[:]))
+        pick_words(0, "x_code_0")
+        first = deal(nc.vector.tensor_copy, w1_raw[0], slice(0, 2), "w1_bf_a", "w1_bf_a")
+        second = deal(nc.scalar.copy, w1_raw[0], slice(2, 4), "w1_bf_b", "w1_bf_b")
+        w1_q.extend(blocks(quantize(first, P, "w1_a")))
+        w1_q.extend(blocks(quantize(second, P, "w1_b")))
+        pick_words(1, "w1_bf_a")
+        gates[0] = keep.tile([P, 4, BANK], F32, name="gates_0", tag="w1_raw_0", align_bytes=64)
+        gates[1] = keep.tile([P, 4, BANK], F32, name="gates_1")
+        for h in range(2):
+            for b in range(2):
+                gate(b, h)
+                scores(b, h)
+        w2_bf = deal(nc.scalar.copy, w2_raw[1], whole, "w2_bf_1", "words")
+        w1_bf = deal(nc.scalar.copy, w1_raw[1], whole, "w1_bf_1", "w2_raw_1")
+
+        first_max(0)
+        w2_q.extend(blocks(quantize(w2_bf, HALF, "w2_1")))
+        second_max(0)
+        for b in range(2, 4):
+            gate(b, 0)
+            gate(b, 1)
+        first_max(1)
+        w1_q.extend(blocks(quantize(w1_bf, HALF, "w1_1")))
+        second_max(1)
+        scores(2, 0)
+        scores(2, 1)
+        scores(3, 0)
+        first_max(2)
+        scores(3, 1)
+        second_max(2)
+        first_max(3)
+
+        bounded = keep.tile([P, PACK, U], F32, name="bounded", tag="w2_1_code", align_bytes=64)
+        factor = keep.tile([P, PACK, U], F32, name="factor")
+        w3_bf = keep.tile([P, N, PACK], BF16, name="w3_bf", tag="w2_1_scale", align_bytes=64)
+        nc.scalar.copy(
+            w3_bf[:].rearrange("p (c i) j -> p c j i", i=2), w3_raw[:].rearrange("p j (c i) -> p c j i", i=2)
+        )
+        look_up(1)
+        second_max(3)
+        for t in range(PACK):
+            nc.scalar.activation(bounded[:, t, :], qry_raw[:, t, :], ACT.Tanh)
+            nc.scalar.activation(factor[:, t, :], bounded[:, t, :], ACT.Copy, scale=unit_t[:, t : t + 1])
         w3_code, w3_scale = quantize(w3_bf[:].rearrange("p n j -> p (n j)"), N, "w3")
-        look_up(PACK - 1)
+        for t in (3, 0, 2):
+            look_up(t)
 
         chunks = range(U // CHUNK)
         hid = []

@@ -50,10 +50,9 @@ def tile_picked_yxindx_tied_p_kernel(tc, x_words, x_scales, w1, w2, qry, unit, w
 
         nc.sync.dma_start(offs_t[:], offs)
         w2_raw = [load_half(w2, 0, "w2_raw_0")]
-        for q in range(4):
-            nc.sync.dma_start(
-                scales[32 * q : 32 * q + 4, :].bitcast(I32), x_scales[0, 4 * q : 4 * q + 4, :].bitcast(I32)
-            )
+        scale_rows = x_scales[0].bitcast(I32).rearrange("(q r) c -> r q c", r=4)
+        for r in range(4):
+            nc.sync.dma_start(scales[:].bitcast(I32)[r:P:32, :], scale_rows[r])
         nc.sync.dma_start(words[:], x_words[0].rearrange("p c r -> p (c r)").bitcast(I32))
         w1_raw = [load_half(w1, 0, "w1_raw_0")]
         w2_raw.append(load_half(w2, 1, "w2_raw_1"))
@@ -70,12 +69,12 @@ def tile_picked_yxindx_tied_p_kernel(tc, x_words, x_scales, w1, w2, qry, unit, w
 
         def deal(copy, raw, slots, name, tag):
             count = slots.stop - slots.start
-            dealt = keep.tile([P, count, HALF // PACK, PACK], BF16, name=name, tag=tag, align_bytes=64)
+            dealt = keep.tile([P, count, 2, HALF // PACK, PACK], BF16, name=name, tag=tag, align_bytes=64)
             copy(
-                dealt[:].rearrange("p t m j -> p m j t"),
-                raw[:].rearrange("p j (m t) -> p m j t", t=PACK)[:, :, :, slots],
+                dealt[:].rearrange("p e u m j -> p e m j u"),
+                raw[:].rearrange("p j (m e u) -> p e m j u", e=2, u=2)[:, slots, :, :, :],
             )
-            return dealt[:].rearrange("p t m j -> p (t m j)")
+            return dealt[:].rearrange("p e u m j -> p (e u m j)")
 
         def quantize(src, width, name):
             code = keep.tile([P, width], U32, name=name + "_code", tag=name + "_code", align_bytes=64)
@@ -154,12 +153,13 @@ def tile_picked_yxindx_tied_p_kernel(tc, x_words, x_scales, w1, w2, qry, unit, w
             at = PLACE[t] * V
             nc.vector.tensor_copy(looked[:, t, :], best[:, at : at + WINDOW].indirect(pg_t[:]))
 
-        whole = slice(0, PACK)
-        w2_q.extend(blocks(quantize(deal(nc.vector.tensor_copy, w2_raw[0], whole, "w2_bf_0", "w2_bf_0"), HALF, "w2_0")))
+        whole = slice(0, 2)
+        w2_bf = deal(nc.scalar.copy, w2_raw[0], whole, "w2_bf_0", "w2_bf_0")
         nc.vector.tensor_copy(x_scale[:], scales[:].indirect(offs_t[:]))
+        w2_q.extend(blocks(quantize(w2_bf, HALF, "w2_0")))
         pick_words(0, "x_code_0")
-        first = deal(nc.vector.tensor_copy, w1_raw[0], slice(0, 2), "w1_bf_a", "w1_bf_a")
-        second = deal(nc.scalar.copy, w1_raw[0], slice(2, 4), "w1_bf_b", "w1_bf_b")
+        first = deal(nc.vector.tensor_copy, w1_raw[0], slice(0, 1), "w1_bf_a", "w1_bf_a")
+        second = deal(nc.scalar.copy, w1_raw[0], slice(1, 2), "w1_bf_b", "w1_bf_b")
         w1_q.extend(blocks(quantize(first, P, "w1_a")))
         w1_q.extend(blocks(quantize(second, P, "w1_b")))
         pick_words(1, "w1_bf_a")

@@ -18,10 +18,9 @@ ACT = mybir.ActivationFunctionType
 P = 128
 PACK = 4
 BANK = 512
-WINDOW = 704
+WINDOW = V + 16
 CHUNK = 256
 HALF = H // 2
-PLACE = {2: 0, 0: 1, 3: 2, 1: 3}
 
 
 def tile_picked_yxindx_tied_p_kernel(tc, x_words, x_scales, w1, w2, qry, unit, w3, old, offs, pg, out):
@@ -35,12 +34,13 @@ def tile_picked_yxindx_tied_p_kernel(tc, x_words, x_scales, w1, w2, qry, unit, w
         pg_t = keep.tile([P, U // 16], U16, name="pg_t")
         words = keep.tile([P, T], I32, name="words", tag="words", align_bytes=64)
         scales = keep.tile([P, T], U8, name="scales", align_bytes=64)
-        best = keep.tile([P, (PACK - 1) * V + WINDOW], F32, name="best", align_bytes=64)
+        best = [keep.tile([P, WINDOW], F32, name="best_%d" % t, align_bytes=64) for t in range(PACK)]
         warm = keep.tile([P, 2], F32, name="warm")
 
         nc.vector.memset(scales[:].bitcast(I32), 0)
         nc.vector.memset(warm[:, 0:1], 0.0)
-        nc.vector.memset(best[:, PACK * V :], 0.0)
+        for t in range(PACK):
+            nc.vector.memset(best[t][:, V:], 0.0)
         nc.scalar.activation(warm[:, 1:2], warm[:, 0:1], ACT.Sigmoid)
 
         def load_half(w, half, name):
@@ -131,27 +131,18 @@ def tile_picked_yxindx_tied_p_kernel(tc, x_words, x_scales, w1, w2, qry, unit, w
             pairs[b] = ring.tile([P, V, 2], F32, name="pairs")
             nc.vector.tensor_tensor(pairs[b][:], score[b][:, :, 0:2], score[b][:, :, 2:4], ALU.max)
 
-        def columns(t):
-            return slice(PLACE[t] * V, (PLACE[t] + 1) * V)
-
         low, high = slice(0, P // 2), slice(P // 2, P)
 
         def second_max(b):
-            even, odd = columns(2 * (b % 2)), columns(2 * (b % 2) + 1)
+            even, odd = best[2 * (b % 2)], best[2 * (b % 2) + 1]
             if b < 2:
-                nc.vector.tensor_tensor(best[:, even], pairs[b][:, :, 0], pairs[b][:, :, 1], ALU.max)
-                nc.sync.dma_start(best[low, odd], best[high, even])
+                nc.vector.tensor_tensor(even[:, :V], pairs[b][:, :, 0], pairs[b][:, :, 1], ALU.max)
+                nc.sync.dma_start(odd[low, :V], even[high, :V])
             else:
                 upper = ring.tile([P, V], F32, name="upper")
                 nc.vector.tensor_tensor(upper[:], pairs[b][:, :, 0], pairs[b][:, :, 1], ALU.max)
-                nc.sync.dma_start(best[high, even], upper[low, :])
-                nc.scalar.copy(best[high, odd], upper[high, :])
-
-        looked = keep.tile([P, PACK, U], F32, name="looked")
-
-        def look_up(t):
-            at = PLACE[t] * V
-            nc.vector.tensor_copy(looked[:, t, :], best[:, at : at + WINDOW].indirect(pg_t[:]))
+                nc.sync.dma_start(even[high, :V], upper[low, :])
+                nc.scalar.copy(odd[high, :V], upper[high, :])
 
         whole = slice(0, 2)
         w2_bf = deal(nc.scalar.copy, w2_raw[0], whole, "w2_bf_0", "w2_bf_0")
@@ -170,7 +161,8 @@ def tile_picked_yxindx_tied_p_kernel(tc, x_words, x_scales, w1, w2, qry, unit, w
                 gate(b, h)
                 scores(b, h)
         w2_bf = deal(nc.scalar.copy, w2_raw[1], whole, "w2_bf_1", "words")
-        w1_bf = deal(nc.scalar.copy, w1_raw[1], whole, "w1_bf_1", "w2_raw_1")
+        third = deal(nc.scalar.copy, w1_raw[1], slice(0, 1), "w1_bf_c", "w2_raw_1")
+        fourth = deal(nc.scalar.copy, w1_raw[1], slice(1, 2), "w1_bf_d", "w1_bf_b")
 
         first_max(0)
         w2_q.extend(blocks(quantize(w2_bf, HALF, "w2_1")))
@@ -178,8 +170,9 @@ def tile_picked_yxindx_tied_p_kernel(tc, x_words, x_scales, w1, w2, qry, unit, w
         for b in range(2, 4):
             gate(b, 0)
             gate(b, 1)
+        w1_q.extend(blocks(quantize(third, P, "w1_c")))
         first_max(1)
-        w1_q.extend(blocks(quantize(w1_bf, HALF, "w1_1")))
+        w1_q.extend(blocks(quantize(fourth, P, "w1_d")))
         second_max(1)
         scores(2, 0)
         scores(2, 1)
@@ -192,28 +185,40 @@ def tile_picked_yxindx_tied_p_kernel(tc, x_words, x_scales, w1, w2, qry, unit, w
         bounded = keep.tile([P, PACK, U], F32, name="bounded", tag="w2_1_code", align_bytes=64)
         factor = keep.tile([P, PACK, U], F32, name="factor")
         w3_bf = keep.tile([P, N, PACK], BF16, name="w3_bf", tag="w2_1_scale", align_bytes=64)
-        nc.scalar.copy(
-            w3_bf[:].rearrange("p (c i) j -> p c j i", i=2), w3_raw[:].rearrange("p j (c i) -> p c j i", i=2)
-        )
-        look_up(1)
-        second_max(3)
-        for t in range(PACK):
+        chunks = range(U // CHUNK)
+        hid_rows = [keep.tile([P, PACK, CHUNK], F32, name="hid_rows_%d" % c) for c in chunks]
+
+        def make_factor(t):
             nc.scalar.activation(bounded[:, t, :], qry_raw[:, t, :], ACT.Tanh)
             nc.scalar.activation(factor[:, t, :], bounded[:, t, :], ACT.Copy, scale=unit_t[:, t : t + 1])
+
+        def look_up(t, c):
+            part = pg_t[:, c * CHUNK // 16 : (c + 1) * CHUNK // 16]
+            nc.vector.tensor_tensor(
+                hid_rows[c][:, t, :], best[t][:].indirect(part), factor[:, t, c * CHUNK : (c + 1) * CHUNK], ALU.mult
+            )
+
+        make_factor(1)
+        look_up(1, 0)
+        second_max(3)
+        look_up(1, 1)
+        make_factor(3)
+        nc.scalar.copy(
+            w3_bf[:].rearrange("p (c i) j -> p c j i", i=4), w3_raw[:].rearrange("p j (c i) -> p c j i", i=4)
+        )
+        make_factor(0)
+        make_factor(2)
         w3_code, w3_scale = quantize(w3_bf[:].rearrange("p n j -> p (n j)"), N, "w3")
         for t in (3, 0, 2):
-            look_up(t)
+            for c in chunks:
+                look_up(t, c)
 
-        chunks = range(U // CHUNK)
         hid = []
-        for c in chunks:
-            cols = slice(c * CHUNK, (c + 1) * CHUNK)
+        for c, copy in zip(chunks, (nc.scalar.copy, nc.vector.tensor_copy)):
             hid.append(keep.tile([P, CHUNK, PACK], BF16, name="hid_%d" % c, align_bytes=64))
-            nc.vector.tensor_tensor(
-                hid[c][:].rearrange("p (c i) t -> p c t i", i=2),
-                looked[:, :, cols].rearrange("p t (c i) -> p c t i", i=2),
-                factor[:, :, cols].rearrange("p t (c i) -> p c t i", i=2),
-                ALU.mult,
+            copy(
+                hid[c][:].rearrange("p (c i) t -> p c t i", i=4),
+                hid_rows[c][:].rearrange("p t (c i) -> p c t i", i=4),
             )
         hid_q = [quantize(hid[c][:].rearrange("p r t -> p (r t)"), CHUNK, "hid_%d" % c) for c in chunks]
         for c in chunks:

@@ -20,6 +20,7 @@ PACK = 4
 BANK = 512
 WINDOW = V + 16
 CHUNK = 256
+PAGES = BANK // D
 HALF = H // 2
 
 
@@ -110,37 +111,40 @@ def tile_picked_yxindx_tied_p_kernel(tc, x_words, x_scales, w1, w2, qry, unit, w
 
         w1_q, w2_q, gates, score, pairs = [], [], {}, {}, {}
 
+        def by_member(acc):
+            return acc[:].rearrange("p (v d) -> p d v", d=D)
+
         def gate(b, h):
             yw = product(w2_q[b], h, "yw", 2)
-            nc.scalar.activation(gates[b // 2][:, 2 * (b % 2) + h, :], yw[:], ACT.Sigmoid)
+            nc.scalar.activation(gates[b // 2][:, 2 * (b % 2) + h, :, :], by_member(yw), ACT.Sigmoid)
 
         def scores(b, h):
             if h == 0:
-                score[b] = ring.tile([P, V, D], F32, name="score")
+                score[b] = ring.tile([P, D, V], F32, name="score")
             ys = product(w1_q[b], h, "ys", 4)
             nc.vector.scalar_tensor_tensor(
-                score[b][:].rearrange("p v d -> p (v d)")[:, h * BANK : (h + 1) * BANK],
-                ys[:],
+                score[b][:, :, h * PAGES : (h + 1) * PAGES],
+                by_member(ys),
                 0.0,
-                gates[b // 2][:, 2 * (b % 2) + h, :],
+                gates[b // 2][:, 2 * (b % 2) + h, :, :],
                 ALU.max,
                 ALU.mult,
             )
 
         def first_max(b):
-            pairs[b] = ring.tile([P, V, 2], F32, name="pairs")
-            nc.vector.tensor_tensor(pairs[b][:], score[b][:, :, 0:2], score[b][:, :, 2:4], ALU.max)
+            pairs[b] = ring.tile([P, 2, V], F32, name="pairs")
+            nc.vector.tensor_tensor(pairs[b][:], score[b][:, 0:2, :], score[b][:, 2:4, :], ALU.max)
 
         low, high = slice(0, P // 2), slice(P // 2, P)
 
         def second_max(b):
             even, odd = best[2 * (b % 2)], best[2 * (b % 2) + 1]
             if b < 2:
-                nc.vector.tensor_tensor(even[:, :V], pairs[b][:, :, 0], pairs[b][:, :, 1], ALU.max)
+                nc.vector.tensor_tensor(even[:, :V], pairs[b][:, 0, :], pairs[b][:, 1, :], ALU.max)
                 nc.sync.dma_start(odd[low, :V], even[high, :V])
             else:
                 upper = ring.tile([P, V], F32, name="upper")
-                nc.vector.tensor_tensor(upper[:], pairs[b][:, :, 0], pairs[b][:, :, 1], ALU.max)
+                nc.vector.tensor_tensor(upper[:], pairs[b][:, 0, :], pairs[b][:, 1, :], ALU.max)
                 nc.sync.dma_start(even[high, :V], upper[low, :])
                 nc.scalar.copy(odd[high, :V], upper[high, :])
 
@@ -154,8 +158,8 @@ def tile_picked_yxindx_tied_p_kernel(tc, x_words, x_scales, w1, w2, qry, unit, w
         w1_q.extend(blocks(quantize(first, P, "w1_a")))
         w1_q.extend(blocks(quantize(second, P, "w1_b")))
         pick_words(1, "w1_bf_a")
-        gates[0] = keep.tile([P, 4, BANK], F32, name="gates_0", tag="w1_raw_0", align_bytes=64)
-        gates[1] = keep.tile([P, 4, BANK], F32, name="gates_1")
+        gates[0] = keep.tile([P, 4, D, PAGES], F32, name="gates_0", tag="w1_raw_0", align_bytes=64)
+        gates[1] = keep.tile([P, 4, D, PAGES], F32, name="gates_1")
         for h in range(2):
             for b in range(2):
                 gate(b, h)

from contextlib import ExitStack

import concourse.mybir as mybir

K, T, S, D, N, H, V, U = 512, 4096, 1024, 4, 128, 512, 256, 512
FLOPS = 2 * K * H * S * 2 + 2 * H * N * U

F32 = mybir.dt.float32
BF16 = mybir.dt.bfloat16
I32 = mybir.dt.int32
U32 = mybir.dt.uint32
U16 = mybir.dt.uint16
U8 = mybir.dt.uint8
FP8X4 = mybir.dt.float8_e4m3fn_x4
ALU = mybir.AluOpType
ACT = mybir.ActivationFunctionType

P = 128
PACK = 4
BANK = 512
WINDOW = V + 16
CHUNK = 256
PAGES = BANK // D
HALF = H // 2


def tile_picked_yxindx_tied_p_kernel(tc, x_words, x_scales, w1, w2, qry, unit, w3, old, offs, pg, out):
    nc = tc.nc
    with ExitStack() as ctx:
        keep = ctx.enter_context(tc.tile_pool(name="keep", bufs=1))
        ring = ctx.enter_context(tc.tile_pool(name="ring", bufs=2))
        psum = ctx.enter_context(tc.psum_pool(name="psum", bufs=1))

        offs_t = keep.tile([P, S // 16], U16, name="offs_t")
        pg_t = keep.tile([P, U // 16], U16, name="pg_t")
        words = keep.tile([P, T], I32, name="words", tag="words", align_bytes=64)
        scales = keep.tile([P, T], U8, name="scales", align_bytes=64)
        best = [keep.tile([P, WINDOW], F32, name="best_%d" % t, align_bytes=64) for t in range(PACK)]
        warm = keep.tile([P, 2], F32, name="warm")

        nc.vector.memset(scales[:].bitcast(I32), 0)
        nc.vector.memset(warm[:, 0:1], 0.0)
        for t in range(PACK):
            nc.vector.memset(best[t][:, V:], 0.0)
        nc.scalar.activation(warm[:, 1:2], warm[:, 0:1], ACT.Sigmoid)

        def load_half(w, half, name):
            raw = keep.tile([P, PACK, HALF], F32, name=name, tag=name, align_bytes=64)
            nc.sync.dma_start(raw[:], w.rearrange("(p j) c -> p j c", j=PACK)[:, :, half * HALF : (half + 1) * HALF])
            return raw

        nc.sync.dma_start(offs_t[:], offs)
        w2_raw = [load_half(w2, 0, "w2_raw_0")]
        scale_rows = x_scales[0].bitcast(I32).rearrange("(q r) c -> r q c", r=4)
        for r in range(4):
            nc.sync.dma_start(scales[:].bitcast(I32)[r:P:32, :], scale_rows[r])
        nc.sync.dma_start(words[:], x_words[0].rearrange("p c r -> p (c r)").bitcast(I32))
        w1_raw = [load_half(w1, 0, "w1_raw_0")]
        w2_raw.append(load_half(w2, 1, "w2_raw_1"))
        w1_raw.append(load_half(w1, 1, "w1_raw_1"))
        qry_raw = keep.tile([P, PACK, U], F32, name="qry_raw")
        w3_raw = keep.tile([P, PACK, N], F32, name="w3_raw")
        unit_t = keep.tile([P, PACK], F32, name="unit_t")
        old_t = keep.tile([P, U], F32, name="old_t")
        nc.sync.dma_start(qry_raw[:], qry.rearrange("(p j) c -> p j c", j=PACK))
        nc.sync.dma_start(unit_t[:], unit.rearrange("(p j) o -> p (j o)", j=PACK))
        nc.sync.dma_start(pg_t[:], pg)
        nc.sync.dma_start(w3_raw[:], w3.rearrange("(p j) c -> p j c", j=PACK))
        nc.sync.dma_start(old_t[:], old)

        def deal(copy, raw, slots, name, tag):
            count = slots.stop - slots.start
            dealt = keep.tile([P, count, 2, HALF // PACK, PACK], BF16, name=name, tag=tag, align_bytes=64)
            copy(
                dealt[:].rearrange("p e u m j -> p e m j u"),
                raw[:].rearrange("p j (m e u) -> p e m j u", e=2, u=2)[:, slots, :, :, :],
            )
            return dealt[:].rearrange("p e u m j -> p (e u m j)")

        def quantize(src, width, name):
            code = keep.tile([P, width], U32, name=name + "_code", tag=name + "_code", align_bytes=64)
            scale = keep.tile([P, width], U8, name=name + "_scale", tag=name + "_scale", align_bytes=64)
            nc.vector.quantize_mx(out=code[:].bitcast(FP8X4), scales=scale[:], in_=src)
            return code, scale

        x_scale = keep.tile([P, S], U8, name="x_scale", align_bytes=64)
        x_code = {}

        def pick_words(h, tag):
            x_code[h] = keep.tile([P, BANK], U32, name="x_code_%d" % h, tag=tag, align_bytes=64)
            part = offs_t[:, h * BANK // 16 : (h + 1) * BANK // 16]
            nc.vector.tensor_copy(x_code[h][:], words[:].bitcast(U32).indirect(part))

        def blocks(quantized):
            code, scale = quantized
            return [(code[:, e * P : (e + 1) * P], scale[:, e * P : (e + 1) * P]) for e in range(code.shape[1] // P)]

        def product(weights, h, tag, bufs):
            code, scale = weights
            acc = psum.tile([P, BANK], F32, name=tag, tag=tag, bufs=bufs)
            nc.tensor.matmul_mx(
                out=acc[:],
                lhsT=code.bitcast(FP8X4),
                lhsT_scale=scale,
                rhs=x_code[h][:].bitcast(FP8X4),
                rhs_scale=x_scale[:, h * BANK : (h + 1) * BANK],
                start=True,
                stop=True,
            )
            return acc

        w1_q, w2_q, gates, score, pairs = [], [], {}, {}, {}

        def by_member(acc):
            return acc[:].rearrange("p (v d) -> p d v", d=D)

        def gate(b, h):
            yw = product(w2_q[b], h, "yw", 2)
            nc.scalar.activation(gates[b // 2][:, 2 * (b % 2) + h, :, :], by_member(yw), ACT.Sigmoid)

        def scores(b, h):
            if h == 0:
                score[b] = ring.tile([P, D, V], F32, name="score")
            ys = product(w1_q[b], h, "ys", 4)
            nc.vector.scalar_tensor_tensor(
                score[b][:, :, h * PAGES : (h + 1) * PAGES],
                by_member(ys),
                0.0,
                gates[b // 2][:, 2 * (b % 2) + h, :, :],
                ALU.max,
                ALU.mult,
            )

        def first_max(b):
            pairs[b] = ring.tile([P, 2, V], F32, name="pairs")
            nc.vector.tensor_tensor(pairs[b][:], score[b][:, 0:2, :], score[b][:, 2:4, :], ALU.max)

        low, high = slice(0, P // 2), slice(P // 2, P)

        def second_max(b):
            even, odd = best[2 * (b % 2)], best[2 * (b % 2) + 1]
            if b < 2:
                nc.vector.tensor_tensor(even[:, :V], pairs[b][:, 0, :], pairs[b][:, 1, :], ALU.max)
                nc.sync.dma_start(odd[low, :V], even[high, :V])
            else:
                upper = ring.tile([P, V], F32, name="upper")
                nc.vector.tensor_tensor(upper[:], pairs[b][:, 0, :], pairs[b][:, 1, :], ALU.max)
                nc.sync.dma_start(even[high, :V], upper[low, :])
                nc.scalar.copy(odd[high, :V], upper[high, :])

        whole = slice(0, 2)
        w2_bf = deal(nc.scalar.copy, w2_raw[0], whole, "w2_bf_0", "w2_bf_0")
        nc.vector.tensor_copy(x_scale[:], scales[:].indirect(offs_t[:]))
        w2_q.extend(blocks(quantize(w2_bf, HALF, "w2_0")))
        pick_words(0, "x_code_0")
        first = deal(nc.vector.tensor_copy, w1_raw[0], slice(0, 1), "w1_bf_a", "w1_bf_a")
        second = deal(nc.scalar.copy, w1_raw[0], slice(1, 2), "w1_bf_b", "w1_bf_b")
        w1_q.extend(blocks(quantize(first, P, "w1_a")))
        w1_q.extend(blocks(quantize(second, P, "w1_b")))
        pick_words(1, "w1_bf_a")
        gates[0] = keep.tile([P, 4, D, PAGES], F32, name="gates_0", tag="w1_raw_0", align_bytes=64)
        gates[1] = keep.tile([P, 4, D, PAGES], F32, name="gates_1")
        for h in range(2):
            for b in range(2):
                gate(b, h)
                scores(b, h)
        w2_bf = deal(nc.scalar.copy, w2_raw[1], whole, "w2_bf_1", "words")
        third = deal(nc.scalar.copy, w1_raw[1], slice(0, 1), "w1_bf_c", "w2_raw_1")
        fourth = deal(nc.scalar.copy, w1_raw[1], slice(1, 2), "w1_bf_d", "w1_bf_b")

        first_max(0)
        w2_q.extend(blocks(quantize(w2_bf, HALF, "w2_1")))
        second_max(0)
        for b in range(2, 4):
            gate(b, 0)
            gate(b, 1)
        w1_q.extend(blocks(quantize(third, P, "w1_c")))
        first_max(1)
        w1_q.extend(blocks(quantize(fourth, P, "w1_d")))
        second_max(1)
        scores(2, 0)
        scores(2, 1)
        scores(3, 0)
        first_max(2)
        scores(3, 1)
        second_max(2)
        first_max(3)

        bounded = keep.tile([P, PACK, U], F32, name="bounded", tag="w2_1_code", align_bytes=64)
        factor = keep.tile([P, PACK, U], F32, name="factor")
        w3_bf = keep.tile([P, N, PACK], BF16, name="w3_bf", tag="w2_1_scale", align_bytes=64)
        chunks = range(U // CHUNK)
        hid_rows = [keep.tile([P, PACK, CHUNK], F32, name="hid_rows_%d" % c) for c in chunks]

        def make_factor(t):
            nc.scalar.activation(bounded[:, t, :], qry_raw[:, t, :], ACT.Tanh)
            nc.scalar.activation(factor[:, t, :], bounded[:, t, :], ACT.Copy, scale=unit_t[:, t : t + 1])

        def look_up(t, c):
            part = pg_t[:, c * CHUNK // 16 : (c + 1) * CHUNK // 16]
            nc.vector.tensor_tensor(
                hid_rows[c][:, t, :], best[t][:].indirect(part), factor[:, t, c * CHUNK : (c + 1) * CHUNK], ALU.mult
            )

        make_factor(1)
        look_up(1, 0)
        second_max(3)
        look_up(1, 1)
        make_factor(3)
        nc.scalar.copy(
            w3_bf[:].rearrange("p (c i) j -> p c j i", i=4), w3_raw[:].rearrange("p j (c i) -> p c j i", i=4)
        )
        make_factor(0)
        make_factor(2)
        w3_code, w3_scale = quantize(w3_bf[:].rearrange("p n j -> p (n j)"), N, "w3")
        for t in (3, 0, 2):
            for c in chunks:
                look_up(t, c)

        hid = []
        for c, copy in zip(chunks, (nc.scalar.copy, nc.vector.tensor_copy)):
            hid.append(keep.tile([P, CHUNK, PACK], BF16, name="hid_%d" % c, align_bytes=64))
            copy(
                hid[c][:].rearrange("p (c i) t -> p c t i", i=4),
                hid_rows[c][:].rearrange("p t (c i) -> p c t i", i=4),
            )
        hid_q = [quantize(hid[c][:].rearrange("p r t -> p (r t)"), CHUNK, "hid_%d" % c) for c in chunks]
        for c in chunks:
            cols = slice(c * CHUNK, (c + 1) * CHUNK)
            rr = psum.tile([P, CHUNK], F32, name="rr", tag="rr", bufs=2)
            nc.tensor.matmul_mx(
                out=rr[:],
                lhsT=w3_code[:].bitcast(FP8X4),
                lhsT_scale=w3_scale[:],
                rhs=hid_q[c][0][:].bitcast(FP8X4),
                rhs_scale=hid_q[c][1][:],
                start=True,
                stop=True,
            )
            res = ring.tile([P, CHUNK], F32, name="res")
            nc.vector.tensor_tensor(res[:], rr[:], old_t[:, cols], ALU.add)
            nc.sync.dma_start(out[:, cols], res[:])
